import numpy as np
import ml_dtypes


def mxq(x, axis, fmt="e4m3"):
    dtype, down = {"e4m3": (ml_dtypes.float8_e4m3fn, 7), "e5m2": (ml_dtypes.float8_e5m2, 14)}[fmt]
    v = np.moveaxis(np.asarray(x, np.float32).astype(ml_dtypes.bfloat16).astype(np.float64), axis, -1)
    blocks = v.reshape(v.shape[:-1] + (-1, 32))
    amax = np.abs(blocks).max(-1, keepdims=True)
    byte = np.maximum(np.where(amax > 0, np.frexp(amax)[1] - 1 + 127, 0) - down, 1)
    scale = np.exp2(byte - 127.0)
    codes = (blocks / scale).astype(np.float32).astype(dtype).astype(np.float64)
    return np.moveaxis((codes * scale).reshape(v.shape), -1, axis)


WIDE = False


def mx_kscale(k):
    if not WIDE:
        return np.ones(k)
    levels = np.array([10, -10, 5, -5, 0])
    if k % 512:
        return np.exp2(np.random.permutation(np.resize(levels, k // 32))).repeat(32)
    a = np.empty((k // 512, 16))
    for p in range(k // 512):
        a[p, :8] = np.random.permutation(np.resize(levels, 8))
        for g in range(8):
            far = levels[np.abs(levels - a[p, g]) >= 10]
            a[p, g + 8] = far[np.random.randint(len(far))]
    return np.exp2(a.ravel()).repeat(32)


def f64(x):
    return np.asarray(x).astype(np.float64)


def striped(idx):
    return np.tile(idx.reshape(-1, 16).T, (8, 1)).astype(np.uint16)


def unstriped(offs):
    return offs[:16].T.reshape(-1).astype(np.int64)


E2M1 = np.array([0.0, 0.5, 1.0, 1.5, 2.0, 3.0, 4.0, 6.0, -0.0, -0.5, -1.0, -1.5, -2.0, -3.0, -4.0, -6.0])


def pack_weight(w, fmt):
    k, n = w.shape
    w = f64(np.asarray(w, np.float32).astype(ml_dtypes.bfloat16)).reshape(k // 32, 32, n)
    amax = np.abs(w).max(1)
    if fmt == "e4m3":
        byte = np.frexp(amax)[1] - 1 + 127 - 7
    else:
        mant, ex = np.frexp(amax / 6.0)
        byte = np.where(mant > 0.5, ex, ex - 1) + 127
    byte = np.clip(np.where(amax > 0, byte, 1), 1, 254)
    scaled = (w * np.exp2(127.0 - byte)[:, None, :]).reshape(k, n).astype(np.float32)
    by_word = np.ascontiguousarray(scaled.reshape(k // 512, 128, 4, n).transpose(0, 1, 3, 2))
    if fmt == "e4m3":
        words = by_word.astype(ml_dtypes.float8_e4m3fn).view(np.uint8)
    else:
        c = by_word.astype(ml_dtypes.float4_e2m1fn).view(np.uint8) & 0xF
        words = (c[..., 0::2] | (c[..., 1::2] << 4)).reshape(k // 512, 128, 2 * n)
    return np.ascontiguousarray(words), np.ascontiguousarray(byte.astype(np.uint8).reshape(k // 512, 16, n))


def unpack_weight(words, scales, fmt):
    g, _, n = scales.shape
    words = np.ascontiguousarray(words).reshape(g, 128, n, -1)
    if fmt == "e4m3":
        vals = words.view(ml_dtypes.float8_e4m3fn).astype(np.float64)
    else:
        nib = np.empty((g, 128, n, 4), np.uint8)
        nib[..., 0::2] = words & 0xF
        nib[..., 1::2] = words >> 4
        vals = E2M1[nib]
    vals = vals * np.repeat(np.exp2(scales.astype(np.float64) - 127.0), 8, axis=1)[..., None]
    return vals.transpose(0, 1, 3, 2).reshape(g * 512, n)


def gelu(v):
    return 0.5 * v * (1.0 + np.tanh(np.sqrt(2.0 / np.pi) * (v + 0.044715 * v**3)))


K, T, S, H, T2, P, N = 1024, 4096, 1024, 512, 2048, 1024, 384

def setup_inputs():
    n = np.random.standard_normal
    s = mx_kscale(K)[:, None]
    u = mx_kscale(H)[:, None]
    tab_words, tab_scales = pack_weight(n((K, T)) * s, "e4m3")
    w2_words, w2_scales = pack_weight(0.5 * n((K, N)) / np.sqrt(K) / s, "e4m3")
    w4_words, w4_scales = pack_weight(n((H, N)) / np.sqrt(H) / u, "e2m1")
    return {
        "tab_words": tab_words, "tab_scales": tab_scales,
        "offs": striped(np.random.permutation(T)[:S]),
        "offs2": striped(np.random.permutation(T2)[:S]),
        "offs3": striped(np.random.permutation(T2)[:P]),
        "offs4": striped(np.random.permutation(T2)[:P]),
        "w1": (n((K, H)) / np.sqrt(K) / s * u.T).astype(np.float32),
        "b1": (0.6 * n(H) * u[:, 0]).astype(np.float32),
        "wgs": np.exp(0.3 * n((128, S))).astype(np.float32),
        "page0": (n((H, T2)) * u).astype(np.float32),
        "w2_words": w2_words, "w2_scales": w2_scales,
        "w4_words": w4_words, "w4_scales": w4_scales,
    }

def reference(tab_words, tab_scales, offs, offs2, offs3, offs4, w1, b1, wgs, page0,
              w2_words, w2_scales, w4_words, w4_scales):
    v = unpack_weight(tab_words, tab_scales, "e4m3")[:, unstriped(offs)]
    w2 = unpack_weight(w2_words, w2_scales, "e4m3")
    w4 = unpack_weight(w4_words, w4_scales, "e2m1")
    h = (mxq(f64(w1), 0, "e4m3").T @ v) + f64(b1)[:, None]
    before = f64(page0)
    page = before.copy()
    page[:, unstriped(offs2)] = np.tile(f64(wgs), (H // 128, 1)) * h
    x = np.maximum(page[:, unstriped(offs3)], before[:, unstriped(offs4)])
    y = w4.T @ mxq(x, 0, "e4m3")
    ph = w2.T @ v
    return y * np.cos(ph)

@@ -1,0 +1,230 @@
+import math
+from contextlib import ExitStack
+
+import concourse.mybir as mybir
+from concourse.masks import make_identity
+
+K, T, S, H, T2, N = 1024, 4096, 1024, 512, 2048, 384
+FLOPS = 2 * K * H * S + 2 * H * N * S + 2 * K * N * S
+
+F32 = mybir.dt.float32
+BF16 = mybir.dt.bfloat16
+I32 = mybir.dt.int32
+U32 = mybir.dt.uint32
+U16 = mybir.dt.uint16
+U8 = mybir.dt.uint8
+FP8X4 = mybir.dt.float8_e4m3fn_x4
+FP4X4 = mybir.dt.float4_e2m1fn_x4
+ALU = mybir.AluOpType
+ACT = mybir.ActivationFunctionType
+
+P = 128
+PACK = 4
+PASSES = K // (P * PACK)
+BANK = 512
+CHUNKS = S // BANK
+BLOCKS = N // P
+PER_COLUMN = 16
+
+
+def tile_list_moth_turnover_scores_kernel(
+    tc, tab_words, tab_scales, offs, offs2, offs3, offs4, w1, b1, wgs, page0,
+    w2_words, w2_scales, w4_words, w4_scales, out,
+):
+    nc = tc.nc
+    with ExitStack() as ctx:
+        keep = ctx.enter_context(tc.tile_pool(name="keep", bufs=1))
+        psum = ctx.enter_context(tc.psum_pool(name="psum", bufs=1))
+
+        def load_list(name, src):
+            lst = keep.tile([P, S // PER_COLUMN], U16, name=name)
+            nc.sync.dma_start(lst[:], src)
+            return lst
+
+        def chunk_of(lst, c):
+            per = BANK // PER_COLUMN
+            return lst[:, c * per : (c + 1) * per]
+
+        def load_scale_rows(queue, plane, scales):
+            rows = PACK * scales.shape[0]
+            for q in range(4):
+                queue.dma_start(
+                    out=plane[32 * q : 32 * q + rows, :].bitcast(I32),
+                    in_=scales[:, 4 * q : 4 * q + 4, :].bitcast(I32),
+                )
+
+        tab_sc = keep.tile([P, T], U8, name="tab_sc", tag="tab_sc", align_bytes=64)
+        nc.vector.memset(tab_sc[:].bitcast(I32), 0)
+        load_scale_rows(nc.gpsimd, tab_sc, tab_scales)
+        w2_sc = keep.tile([P, N], U8, name="w2_sc", align_bytes=64)
+        w4_sc = keep.tile([P, N], U8, name="w4_sc", align_bytes=64)
+        nc.vector.memset(w2_sc[:].bitcast(I32), 0)
+        nc.vector.memset(w4_sc[:].bitcast(I32), 0)
+        ident = keep.tile([P, P], F32, name="ident")
+        make_identity(nc, ident[:])
+
+        w1_raw = [keep.tile([P, PACK, H], F32, name=f"w1_raw{a}") for a in range(PASSES)]
+        tab_w = [keep.tile([P, T], I32, name=f"tab_w{a}", tag=f"tab_w{a}") for a in range(PASSES)]
+        page = [keep.tile([P, T2], F32, name=f"page{t}") for t in range(PACK)]
+        gain = [keep.tile([P, S], F32, name=f"gain{t}", tag=f"gain{t}") for t in range(PACK)]
+        w1_rows = w1.rearrange("(a p i) c -> a p i c", a=PASSES, i=PACK)
+        page_rows = page0.rearrange("(p t) m -> t p m", t=PACK)
+        gain_rows = wgs.rearrange("(m t) j -> t m j", t=PACK)
+
+        def load_gain(t):
+            for q in (0, 2, 1, 3):
+                nc.sync.dma_start(out=gain[t][32 * q : 32 * (q + 1), :], in_=gain_rows[t])
+
+        nc.sync.dma_start(out=w1_raw[0][:], in_=w1_rows[0])
+        idx = load_list("idx", offs)
+        nc.sync.dma_start(out=w1_raw[1][:], in_=w1_rows[1])
+        for a in range(PASSES):
+            nc.sync.dma_start(out=tab_w[a][:], in_=tab_words[a].rearrange("p n i -> p (n i)").bitcast(I32))
+        idx4 = load_list("idx4", offs4)
+        bias = keep.tile([P, PACK], F32, name="bias")
+        nc.sync.dma_start(out=bias[:], in_=b1.rearrange("(p t) -> p t", t=PACK))
+        nc.sync.dma_start(out=page[0][:], in_=page_rows[0])
+        idx2 = load_list("idx2", offs2)
+        nc.sync.dma_start(out=page[1][:], in_=page_rows[1])
+        load_gain(0)
+        nc.sync.dma_start(out=page[2][:], in_=page_rows[2])
+        load_gain(1)
+        w2_w = [keep.tile([P, N], I32, name=f"w2_w{a}", align_bytes=64) for a in range(PASSES)]
+        for a in range(PASSES):
+            nc.sync.dma_start(out=w2_w[a][:], in_=w2_words[a].rearrange("p n i -> p (n i)").bitcast(I32))
+        load_scale_rows(nc.sync, w2_sc, w2_scales)
+        nc.sync.dma_start(out=page[3][:], in_=page_rows[3])
+        load_gain(2)
+        load_gain(3)
+        idx3 = load_list("idx3", offs3)
+        w4_w = keep.tile([P, 2 * N], U8, name="w4_w", align_bytes=64)
+        nc.sync.dma_start(out=w4_w[:].bitcast(I32), in_=w4_words[0].bitcast(I32))
+        load_scale_rows(nc.sync, w4_sc, w4_scales)
+
+        w1_q = [keep.tile([P, H], U32, name=f"w1_q{a}", align_bytes=64) for a in range(PASSES)]
+        w1_s = [keep.tile([P, H], U8, name=f"w1_s{a}", align_bytes=64) for a in range(PASSES)]
+        w1_bf = [keep.tile([P, PACK * H], BF16, name=f"w1_bf{a}", align_bytes=64) for a in range(PASSES)]
+        for a, copy in enumerate((nc.scalar.copy, nc.vector.tensor_copy)):
+            copy(
+                out=w1_bf[a][:].rearrange("p (t m i) -> p t m i", t=PACK, i=PACK),
+                in_=w1_raw[a][:].rearrange("p i (m t) -> p t m i", t=PACK),
+            )
+
+        v_s = keep.tile([P, S], U8, name="v_s", align_bytes=64)
+        nc.vector.tensor_copy(v_s[:], tab_sc[:].indirect(idx[:]))
+        for a in range(PASSES):
+            nc.vector.quantize_mx(out=w1_q[a][:].bitcast(FP8X4), scales=w1_s[a][:], in_=w1_bf[a][:])
+        v_w = [
+            keep.tile([P, S], U32, name=f"v_w{a}", tag=tag, align_bytes=64)
+            for a, tag in enumerate(("tab_sc", "v_w1"))
+        ]
+        nc.vector.tensor_copy(v_w[0][:], tab_w[0][:].bitcast(U32).indirect(idx[:]))
+        for c in range(CHUNKS):
+            nc.vector.tensor_copy(
+                v_w[1][:, c * BANK : (c + 1) * BANK], tab_w[1][:].bitcast(U32).indirect(chunk_of(idx, c))
+            )
+
+        h = [keep.tile([P, S], F32, name=f"h{t}", tag=f"h{t}") for t in range(PACK)]
+        for t in range(PACK):
+            for c in range(CHUNKS):
+                cols = slice(c * BANK, (c + 1) * BANK)
+                acc = psum.tile([P, BANK], F32, name="acc", tag="acc", bufs=4)
+                for a in range(PASSES):
+                    nc.tensor.matmul_mx(
+                        out=acc[:],
+                        lhsT=w1_q[a][:, t * P : (t + 1) * P].bitcast(FP8X4),
+                        lhsT_scale=w1_s[a][:, t * P : (t + 1) * P],
+                        rhs=v_w[a][:, cols].bitcast(FP8X4),
+                        rhs_scale=v_s[PACK * a :, cols],
+                        start=(a == 0),
+                        stop=(a == PASSES - 1),
+                    )
+                nc.scalar.activation(out=h[t][:, cols], in_=acc[:], func=ACT.Identity, bias=bias[:, t : t + 1])
+
+        before = keep.tile([P, PACK, S], F32, name="before", tag="tab_w0")
+
+        def fetch_before(t):
+            nc.vector.tensor_copy(before[:, t, :], page[t][:].indirect(idx4[:]))
+
+        fetch_before(0)
+        for t in range(PACK):
+            if t + 1 < PACK:
+                fetch_before(t + 1)
+            nc.vector.tensor_tensor(page[t][:].indirect(idx2[:]), h[t][:], gain[t][:], ALU.mult)
+
+        twice_sq = keep.tile([P, BLOCKS, S], F32, name="twice_sq")
+        entry_blocks = BANK // P
+        for c in range(CHUNKS):
+            mag = keep.tile([P, entry_blocks, N], F32, name="mag", tag="mag", bufs=2)
+            for e in range(entry_blocks):
+                cols = slice(c * BANK + e * P, c * BANK + (e + 1) * P)
+                ph = psum.tile([P, N], F32, name="ph", tag="ph", bufs=2)
+                for n0, n1 in ((0, 2 * P), (2 * P, N)):
+                    for a in range(PASSES):
+                        nc.tensor.matmul_mx(
+                            out=ph[:, n0:n1],
+                            lhsT=v_w[a][:, cols].bitcast(FP8X4),
+                            lhsT_scale=v_s[PACK * a :, cols],
+                            rhs=w2_w[a][:, n0:n1].bitcast(FP8X4),
+                            rhs_scale=w2_sc[PACK * a :, n0:n1],
+                            start=(a == 0),
+                            stop=(a == PASSES - 1),
+                        )
+                nc.scalar.activation(out=mag[:, e, :], in_=ph[:], func=ACT.Abs)
+            turns = keep.tile([P, entry_blocks, N], U32, name="turns", tag="turns")
+            nc.scalar.activation(out=turns[:], in_=mag[:], func=ACT.Copy, scale=1.0 / (2.0 * math.pi), bias=0.75)
+            shift = keep.tile([P, entry_blocks, N], F32, name="shift", tag="shift")
+            nc.scalar.activation(out=shift[:], in_=turns[:], func=ACT.Copy, scale=-2.0 * math.pi, bias=math.pi)
+            for b in range(BLOCKS):
+                red = psum.tile([P, BANK], F32, name="red", tag="red", bufs=2)
+                for e in range(entry_blocks):
+                    for first, term in ((True, mag), (False, shift)):
+                        nc.tensor.matmul(
+                            out=red[:, e * P : (e + 1) * P],
+                            lhsT=term[:, e, b * P : (b + 1) * P],
+                            rhs=ident[:],
+                            is_transpose=True,
+                            start=first,
+                            stop=not first,
+                        )
+                half_cos = keep.tile([P, BANK], F32, name="half_cos", tag="half_cos", bufs=2)
+                nc.scalar.activation(out=half_cos[:], in_=red[:], func=ACT.Sin, scale=0.5)
+                nc.scalar.activation(
+                    out=twice_sq[:, b, c * BANK : (c + 1) * BANK], in_=half_cos[:], func=ACT.Square, scale=math.sqrt(2.0)
+                )
+
+        x_q, x_s = [], []
+        for c, tag in enumerate((f"gain{PACK - 1}", f"h{PACK - 1}")):
+            after = keep.tile([P, PACK, BANK], F32, name=f"after{c}", tag=tag)
+            for t in range(PACK):
+                nc.vector.tensor_copy(after[:, t, :], page[t][:].indirect(chunk_of(idx3, c)))
+            x_bf = keep.tile([P, PACK * BANK], BF16, name=f"x_bf{c}", align_bytes=64)
+            nc.vector.tensor_tensor(
+                x_bf[:].rearrange("p (g i t) -> p g t i", i=2, t=PACK),
+                after[:].rearrange("p t (g i) -> p g t i", i=2),
+                before[:, :, c * BANK : (c + 1) * BANK].rearrange("p t (g i) -> p g t i", i=2),
+                ALU.max,
+            )
+            codes = keep.tile([P, BANK], U32, name=f"x_q{c}", align_bytes=64)
+            scales = keep.tile([P, BANK], U8, name=f"x_s{c}", align_bytes=64)
+            nc.vector.quantize_mx(out=codes[:].bitcast(FP8X4), scales=scales[:], in_=x_bf[:])
+            x_q.append(codes)
+            x_s.append(scales)
+        for c in range(CHUNKS):
+            cols = slice(c * BANK, (c + 1) * BANK)
+            for b in range(BLOCKS):
+                acc = psum.tile([P, BANK], F32, name="acc", tag="acc", bufs=4)
+                nc.tensor.matmul_mx(
+                    out=acc[:],
+                    lhsT=w4_w[:, 2 * b * P : 2 * (b + 1) * P].bitcast(FP4X4),
+                    lhsT_scale=w4_sc[:, b * P : (b + 1) * P],
+                    rhs=x_q[c][:].bitcast(FP8X4),
+                    rhs_scale=x_s[c][:],
+                    start=True,
+                    stop=True,
+                )
+                score = keep.tile([P, BANK], F32, name="score", tag="score", bufs=4)
+                nc.vector.scalar_tensor_tensor(
+                    score[:], twice_sq[:, b, cols], 1.0, acc[:], ALU.subtract, ALU.mult
+                )
+                nc.sync.dma_start(out=out[b * P : (b + 1) * P, cols], in_=score[:])

@@ -55,7 +55,6 @@ def tile_list_moth_turnover_scores_kernel(
 
         tab_sc = keep.tile([P, T], U8, name="tab_sc", tag="tab_sc", align_bytes=64)
         nc.vector.memset(tab_sc[:].bitcast(I32), 0)
-        load_scale_rows(nc.gpsimd, tab_sc, tab_scales)
         w2_sc = keep.tile([P, N], U8, name="w2_sc", align_bytes=64)
         w4_sc = keep.tile([P, N], U8, name="w4_sc", align_bytes=64)
         nc.vector.memset(w2_sc[:].bitcast(I32), 0)
@@ -76,6 +75,7 @@ def tile_list_moth_turnover_scores_kernel(
                 nc.sync.dma_start(out=gain[t][32 * q : 32 * (q + 1), :], in_=gain_rows[t])
 
         nc.sync.dma_start(out=w1_raw[0][:], in_=w1_rows[0])
+        load_scale_rows(nc.sync, tab_sc, tab_scales)
         idx = load_list("idx", offs)
         nc.sync.dma_start(out=w1_raw[1][:], in_=w1_rows[1])
         for a in range(PASSES):

@@ -41,9 +41,8 @@ def tile_list_moth_turnover_scores_kernel(
             nc.sync.dma_start(lst[:], src)
             return lst
 
-        def chunk_of(lst, c):
-            per = BANK // PER_COLUMN
-            return lst[:, c * per : (c + 1) * per]
+        def entries(lst, cols):
+            return lst[:, cols.start // PER_COLUMN : cols.stop // PER_COLUMN]
 
         def load_scale_rows(queue, plane, scales):
             rows = PACK * scales.shape[0]
@@ -65,14 +64,14 @@ def tile_list_moth_turnover_scores_kernel(
         w1_raw = [keep.tile([P, PACK, H], F32, name=f"w1_raw{a}") for a in range(PASSES)]
         tab_w = [keep.tile([P, T], I32, name=f"tab_w{a}", tag=f"tab_w{a}") for a in range(PASSES)]
         page = [keep.tile([P, T2], F32, name=f"page{t}") for t in range(PACK)]
-        gain = [keep.tile([P, S], F32, name=f"gain{t}", tag=f"gain{t}") for t in range(PACK)]
+        gain = [keep.tile([P, S], F32, name=f"gain{t}", tag=f"gain{t}", align_bytes=64) for t in range(PACK)]
         w1_rows = w1.rearrange("(a p i) c -> a p i c", a=PASSES, i=PACK)
         page_rows = page0.rearrange("(p t) m -> t p m", t=PACK)
         gain_rows = wgs.rearrange("(m t) j -> t m j", t=PACK)
 
-        def load_gain(t):
+        def load_gain(t, cols=slice(0, S)):
             for q in (0, 2, 1, 3):
-                nc.sync.dma_start(out=gain[t][32 * q : 32 * (q + 1), :], in_=gain_rows[t])
+                nc.sync.dma_start(out=gain[t][32 * q : 32 * (q + 1), cols], in_=gain_rows[t][:, cols])
 
         nc.sync.dma_start(out=w1_raw[0][:], in_=w1_rows[0])
         load_scale_rows(nc.sync, tab_sc, tab_scales)
@@ -85,8 +84,9 @@ def tile_list_moth_turnover_scores_kernel(
         nc.sync.dma_start(out=bias[:], in_=b1.rearrange("(p t) -> p t", t=PACK))
         nc.sync.dma_start(out=page[0][:], in_=page_rows[0])
         idx2 = load_list("idx2", offs2)
+        load_gain(0, slice(0, BANK))
         nc.sync.dma_start(out=page[1][:], in_=page_rows[1])
-        load_gain(0)
+        load_gain(0, slice(BANK, S))
         nc.sync.dma_start(out=page[2][:], in_=page_rows[2])
         load_gain(1)
         w2_w = [keep.tile([P, N], I32, name=f"w2_w{a}", align_bytes=64) for a in range(PASSES)]
@@ -120,11 +120,10 @@ def tile_list_moth_turnover_scores_kernel(
         ]
         nc.vector.tensor_copy(v_w[0][:], tab_w[0][:].bitcast(U32).indirect(idx[:]))
         for c in range(CHUNKS):
-            nc.vector.tensor_copy(
-                v_w[1][:, c * BANK : (c + 1) * BANK], tab_w[1][:].bitcast(U32).indirect(chunk_of(idx, c))
-            )
+            cols = slice(c * BANK, (c + 1) * BANK)
+            nc.vector.tensor_copy(v_w[1][:, cols], tab_w[1][:].bitcast(U32).indirect(entries(idx, cols)))
 
-        h = [keep.tile([P, S], F32, name=f"h{t}", tag=f"h{t}") for t in range(PACK)]
+        h = [keep.tile([P, S], F32, name=f"h{t}", tag=f"h{t}", align_bytes=64) for t in range(PACK)]
         for t in range(PACK):
             for c in range(CHUNKS):
                 cols = slice(c * BANK, (c + 1) * BANK)
@@ -146,11 +145,17 @@ def tile_list_moth_turnover_scores_kernel(
         def fetch_before(t):
             nc.vector.tensor_copy(before[:, t, :], page[t][:].indirect(idx4[:]))
 
+        def put(t, cols):
+            nc.vector.tensor_tensor(page[t][:].indirect(entries(idx2, cols)), h[t][:, cols], gain[t][:, cols], ALU.mult)
+
         fetch_before(0)
-        for t in range(PACK):
+        put(0, slice(0, BANK))
+        fetch_before(1)
+        put(0, slice(BANK, S))
+        for t in range(1, PACK):
             if t + 1 < PACK:
                 fetch_before(t + 1)
-            nc.vector.tensor_tensor(page[t][:].indirect(idx2[:]), h[t][:], gain[t][:], ALU.mult)
+            put(t, slice(0, S))
 
         twice_sq = keep.tile([P, BLOCKS, S], F32, name="twice_sq")
         entry_blocks = BANK // P
@@ -193,27 +198,29 @@ def tile_list_moth_turnover_scores_kernel(
                     out=twice_sq[:, b, c * BANK : (c + 1) * BANK], in_=half_cos[:], func=ACT.Square, scale=math.sqrt(2.0)
                 )
 
+        spans = (slice(0, 512), slice(512, 768), slice(768, 1024))
+        after_tags = (f"gain{PACK - 1}", f"h{PACK - 1}", "x_bf0")
         x_q, x_s = [], []
-        for c, tag in enumerate((f"gain{PACK - 1}", f"h{PACK - 1}")):
-            after = keep.tile([P, PACK, BANK], F32, name=f"after{c}", tag=tag)
+        for c, cols in enumerate(spans):
+            width = cols.stop - cols.start
+            picked = keep.tile([P, PACK, width], F32, name=f"after{c}", tag=after_tags[c], align_bytes=64)
             for t in range(PACK):
-                nc.vector.tensor_copy(after[:, t, :], page[t][:].indirect(chunk_of(idx3, c)))
-            x_bf = keep.tile([P, PACK * BANK], BF16, name=f"x_bf{c}", align_bytes=64)
-            nc.vector.tensor_tensor(
-                x_bf[:].rearrange("p (g i t) -> p g t i", i=2, t=PACK),
-                after[:].rearrange("p t (g i) -> p g t i", i=2),
-                before[:, :, c * BANK : (c + 1) * BANK].rearrange("p t (g i) -> p g t i", i=2),
-                ALU.max,
+                nc.vector.tensor_copy(picked[:, t, :], page[t][:].indirect(entries(idx3, cols)))
+            planes = keep.tile([P, PACK, width], BF16, name=f"planes{c}")
+            nc.vector.tensor_tensor(planes[:], picked[:], before[:, :, cols], ALU.max)
+            x_bf = keep.tile([P, width, PACK], BF16, name=f"x_bf{c}", tag=f"x_bf{c}", align_bytes=64)
+            nc.scalar.copy(out=x_bf[:], in_=planes[:].rearrange("p t j -> p j t"))
+            codes = keep.tile([P, width], U32, name=f"x_q{c}", align_bytes=64)
+            scales = keep.tile([P, width], U8, name=f"x_s{c}", align_bytes=64)
+            nc.vector.quantize_mx(
+                out=codes[:].bitcast(FP8X4), scales=scales[:], in_=x_bf[:].rearrange("p j t -> p (j t)")
             )
-            codes = keep.tile([P, BANK], U32, name=f"x_q{c}", align_bytes=64)
-            scales = keep.tile([P, BANK], U8, name=f"x_s{c}", align_bytes=64)
-            nc.vector.quantize_mx(out=codes[:].bitcast(FP8X4), scales=scales[:], in_=x_bf[:])
             x_q.append(codes)
             x_s.append(scales)
-        for c in range(CHUNKS):
-            cols = slice(c * BANK, (c + 1) * BANK)
+        for c, cols in enumerate(spans):
+            width = cols.stop - cols.start
             for b in range(BLOCKS):
-                acc = psum.tile([P, BANK], F32, name="acc", tag="acc", bufs=4)
+                acc = psum.tile([P, width], F32, name="acc", tag="acc", bufs=4)
                 nc.tensor.matmul_mx(
                     out=acc[:],
                     lhsT=w4_w[:, 2 * b * P : 2 * (b + 1) * P].bitcast(FP4X4),
@@ -223,7 +230,7 @@ def tile_list_moth_turnover_scores_kernel(
                     start=True,
                     stop=True,
                 )
-                score = keep.tile([P, BANK], F32, name="score", tag="score", bufs=4)
+                score = keep.tile([P, width], F32, name="score", tag="score", bufs=6)
                 nc.vector.scalar_tensor_tensor(
                     score[:], twice_sq[:, b, cols], 1.0, acc[:], ALU.subtract, ALU.mult
                 )

@@ -176,9 +176,9 @@ def tile_list_moth_turnover_scores_kernel(
                             stop=(a == PASSES - 1),
                         )
                 nc.scalar.activation(out=mag[:, e, :], in_=ph[:], func=ACT.Abs)
-            turns = keep.tile([P, entry_blocks, N], U32, name="turns", tag="turns")
+            turns = keep.tile([P, entry_blocks, N], U32, name="turns", tag="turns", bufs=2)
             nc.scalar.activation(out=turns[:], in_=mag[:], func=ACT.Copy, scale=1.0 / (2.0 * math.pi), bias=0.75)
-            shift = keep.tile([P, entry_blocks, N], F32, name="shift", tag="shift")
+            shift = keep.tile([P, entry_blocks, N], F32, name="shift", tag="shift", bufs=2)
             nc.scalar.activation(out=shift[:], in_=turns[:], func=ACT.Copy, scale=-2.0 * math.pi, bias=math.pi)
             for b in range(BLOCKS):
                 red = psum.tile([P, BANK], F32, name="red", tag="red", bufs=2)
@@ -192,23 +192,26 @@ def tile_list_moth_turnover_scores_kernel(
                             start=first,
                             stop=not first,
                         )
-                half_cos = keep.tile([P, BANK], F32, name="half_cos", tag="half_cos", bufs=2)
+                half_cos = keep.tile([P, BANK], F32, name="half_cos", tag=("half_cos", "x_bf0")[(c * BLOCKS + b) % 2], align_bytes=64)
                 nc.scalar.activation(out=half_cos[:], in_=red[:], func=ACT.Sin, scale=0.5)
                 nc.scalar.activation(
                     out=twice_sq[:, b, c * BANK : (c + 1) * BANK], in_=half_cos[:], func=ACT.Square, scale=math.sqrt(2.0)
                 )
 
-        spans = (slice(0, 512), slice(512, 768), slice(768, 1024))
-        after_tags = (f"gain{PACK - 1}", f"h{PACK - 1}", "x_bf0")
+        spans = (slice(0, 256), slice(256, 768), slice(768, 1024))
+        after_tags = (f"gain{PACK - 1}", f"h{PACK - 1}", f"gain{PACK - 1}")
+        score_tags = ("planes0", "score1", "score2")
+        woven_tags = ("x_bf0", "planes0", "planes1")
+        banks = [("acc", 4)] * 4 + [("red", 2)] * 2 + [("ph", 2)] * 2
         x_q, x_s = [], []
         for c, cols in enumerate(spans):
             width = cols.stop - cols.start
             picked = keep.tile([P, PACK, width], F32, name=f"after{c}", tag=after_tags[c], align_bytes=64)
             for t in range(PACK):
                 nc.vector.tensor_copy(picked[:, t, :], page[t][:].indirect(entries(idx3, cols)))
-            planes = keep.tile([P, PACK, width], BF16, name=f"planes{c}")
+            planes = keep.tile([P, PACK, width], BF16, name=f"planes{c}", tag=f"planes{c}", align_bytes=64)
             nc.vector.tensor_tensor(planes[:], picked[:], before[:, :, cols], ALU.max)
-            x_bf = keep.tile([P, width, PACK], BF16, name=f"x_bf{c}", tag=f"x_bf{c}", align_bytes=64)
+            x_bf = keep.tile([P, width, PACK], BF16, name=f"x_bf{c}", tag=woven_tags[c], align_bytes=64)
             nc.scalar.copy(out=x_bf[:], in_=planes[:].rearrange("p t j -> p j t"))
             codes = keep.tile([P, width], U32, name=f"x_q{c}", align_bytes=64)
             scales = keep.tile([P, width], U8, name=f"x_s{c}", align_bytes=64)
@@ -219,8 +222,10 @@ def tile_list_moth_turnover_scores_kernel(
             x_s.append(scales)
         for c, cols in enumerate(spans):
             width = cols.stop - cols.start
+            score = keep.tile([P, BLOCKS, width], F32, name=f"score{c}", tag=score_tags[c], align_bytes=64)
             for b in range(BLOCKS):
-                acc = psum.tile([P, width], F32, name="acc", tag="acc", bufs=4)
+                tag, bufs = banks[(c * BLOCKS + b) % len(banks)]
+                acc = psum.tile([P, width], F32, name="y", tag=tag, bufs=bufs)
                 nc.tensor.matmul_mx(
                     out=acc[:],
                     lhsT=w4_w[:, 2 * b * P : 2 * (b + 1) * P].bitcast(FP4X4),
@@ -230,8 +235,7 @@ def tile_list_moth_turnover_scores_kernel(
                     start=True,
                     stop=True,
                 )
-                score = keep.tile([P, width], F32, name="score", tag="score", bufs=6)
                 nc.vector.scalar_tensor_tensor(
-                    score[:], twice_sq[:, b, cols], 1.0, acc[:], ALU.subtract, ALU.mult
+                    score[:, b, :], twice_sq[:, b, cols], 1.0, acc[:], ALU.subtract, ALU.mult
                 )
-                nc.sync.dma_start(out=out[b * P : (b + 1) * P, cols], in_=score[:])
+                nc.sync.dma_start(out=out[b * P : (b + 1) * P, cols], in_=score[:, b, :])

import math
from contextlib import ExitStack

import concourse.mybir as mybir
from concourse.masks import make_identity

K, T, S, H, T2, N = 1024, 4096, 1024, 512, 2048, 384
FLOPS = 2 * K * H * S + 2 * H * N * S + 2 * K * N * S

F32 = mybir.dt.float32
BF16 = mybir.dt.bfloat16
I32 = mybir.dt.int32
U32 = mybir.dt.uint32
U16 = mybir.dt.uint16
U8 = mybir.dt.uint8
FP8X4 = mybir.dt.float8_e4m3fn_x4
FP4X4 = mybir.dt.float4_e2m1fn_x4
ALU = mybir.AluOpType
ACT = mybir.ActivationFunctionType

P = 128
PACK = 4
PASSES = K // (P * PACK)
BANK = 512
CHUNKS = S // BANK
BLOCKS = N // P
PER_COLUMN = 16


def tile_list_moth_turnover_scores_kernel(
    tc, tab_words, tab_scales, offs, offs2, offs3, offs4, w1, b1, wgs, page0,
    w2_words, w2_scales, w4_words, w4_scales, out,
):
    nc = tc.nc
    with ExitStack() as ctx:
        keep = ctx.enter_context(tc.tile_pool(name="keep", bufs=1))
        psum = ctx.enter_context(tc.psum_pool(name="psum", bufs=1))

        def load_list(name, src):
            lst = keep.tile([P, S // PER_COLUMN], U16, name=name)
            nc.sync.dma_start(lst[:], src)
            return lst

        def entries(lst, cols):
            return lst[:, cols.start // PER_COLUMN : cols.stop // PER_COLUMN]

        def load_scale_rows(queue, plane, scales):
            rows = PACK * scales.shape[0]
            for q in range(4):
                queue.dma_start(
                    out=plane[32 * q : 32 * q + rows, :].bitcast(I32),
                    in_=scales[:, 4 * q : 4 * q + 4, :].bitcast(I32),
                )

        tab_sc = keep.tile([P, T], U8, name="tab_sc", tag="tab_sc", align_bytes=64)
        nc.vector.memset(tab_sc[:].bitcast(I32), 0)
        w2_sc = keep.tile([P, N], U8, name="w2_sc", align_bytes=64)
        w4_sc = keep.tile([P, N], U8, name="w4_sc", align_bytes=64)
        nc.vector.memset(w2_sc[:].bitcast(I32), 0)
        nc.vector.memset(w4_sc[:].bitcast(I32), 0)
        ident = keep.tile([P, P], F32, name="ident")
        make_identity(nc, ident[:])

        w1_raw = [keep.tile([P, PACK, H], F32, name=f"w1_raw{a}") for a in range(PASSES)]
        tab_w = [keep.tile([P, T], I32, name=f"tab_w{a}", tag=f"tab_w{a}") for a in range(PASSES)]
        page = [keep.tile([P, T2], F32, name=f"page{t}") for t in range(PACK)]
        gain = [keep.tile([P, S], F32, name=f"gain{t}", tag=f"gain{t}", align_bytes=64) for t in range(PACK)]
        w1_rows = w1.rearrange("(a p i) c -> a p i c", a=PASSES, i=PACK)
        page_rows = page0.rearrange("(p t) m -> t p m", t=PACK)
        gain_rows = wgs.rearrange("(m t) j -> t m j", t=PACK)

        def load_gain(t, cols=slice(0, S)):
            for q in (0, 2, 1, 3):
                nc.sync.dma_start(out=gain[t][32 * q : 32 * (q + 1), cols], in_=gain_rows[t][:, cols])

        nc.sync.dma_start(out=w1_raw[0][:], in_=w1_rows[0])
        load_scale_rows(nc.sync, tab_sc, tab_scales)
        idx = load_list("idx", offs)
        nc.sync.dma_start(out=w1_raw[1][:], in_=w1_rows[1])
        for a in range(PASSES):
            nc.sync.dma_start(out=tab_w[a][:], in_=tab_words[a].rearrange("p n i -> p (n i)").bitcast(I32))
        idx4 = load_list("idx4", offs4)
        bias = keep.tile([P, PACK], F32, name="bias")
        nc.sync.dma_start(out=bias[:], in_=b1.rearrange("(p t) -> p t", t=PACK))
        nc.sync.dma_start(out=page[0][:], in_=page_rows[0])
        idx2 = load_list("idx2", offs2)
        load_gain(0, slice(0, BANK))
        nc.sync.dma_start(out=page[1][:], in_=page_rows[1])
        load_gain(0, slice(BANK, S))
        nc.sync.dma_start(out=page[2][:], in_=page_rows[2])
        load_gain(1)
        w2_w = [keep.tile([P, N], I32, name=f"w2_w{a}", align_bytes=64) for a in range(PASSES)]
        for a in range(PASSES):
            nc.sync.dma_start(out=w2_w[a][:], in_=w2_words[a].rearrange("p n i -> p (n i)").bitcast(I32))
        load_scale_rows(nc.sync, w2_sc, w2_scales)
        nc.sync.dma_start(out=page[3][:], in_=page_rows[3])
        load_gain(2)
        load_gain(3)
        idx3 = load_list("idx3", offs3)
        w4_w = keep.tile([P, 2 * N], U8, name="w4_w", align_bytes=64)
        nc.sync.dma_start(out=w4_w[:].bitcast(I32), in_=w4_words[0].bitcast(I32))
        load_scale_rows(nc.sync, w4_sc, w4_scales)

        w1_q = [keep.tile([P, H], U32, name=f"w1_q{a}", align_bytes=64) for a in range(PASSES)]
        w1_s = [keep.tile([P, H], U8, name=f"w1_s{a}", align_bytes=64) for a in range(PASSES)]
        w1_bf = [keep.tile([P, PACK * H], BF16, name=f"w1_bf{a}", align_bytes=64) for a in range(PASSES)]
        for a, copy in enumerate((nc.scalar.copy, nc.vector.tensor_copy)):
            copy(
                out=w1_bf[a][:].rearrange("p (t m i) -> p t m i", t=PACK, i=PACK),
                in_=w1_raw[a][:].rearrange("p i (m t) -> p t m i", t=PACK),
            )

        v_s = keep.tile([P, S], U8, name="v_s", align_bytes=64)
        nc.vector.tensor_copy(v_s[:], tab_sc[:].indirect(idx[:]))
        for a in range(PASSES):
            nc.vector.quantize_mx(out=w1_q[a][:].bitcast(FP8X4), scales=w1_s[a][:], in_=w1_bf[a][:])
        v_w = [
            keep.tile([P, S], U32, name=f"v_w{a}", tag=tag, align_bytes=64)
            for a, tag in enumerate(("tab_sc", "v_w1"))
        ]
        nc.vector.tensor_copy(v_w[0][:], tab_w[0][:].bitcast(U32).indirect(idx[:]))
        for c in range(CHUNKS):
            cols = slice(c * BANK, (c + 1) * BANK)
            nc.vector.tensor_copy(v_w[1][:, cols], tab_w[1][:].bitcast(U32).indirect(entries(idx, cols)))

        h = [keep.tile([P, S], F32, name=f"h{t}", tag=f"h{t}", align_bytes=64) for t in range(PACK)]
        for t in range(PACK):
            for c in range(CHUNKS):
                cols = slice(c * BANK, (c + 1) * BANK)
                acc = psum.tile([P, BANK], F32, name="acc", tag="acc", bufs=4)
                for a in range(PASSES):
                    nc.tensor.matmul_mx(
                        out=acc[:],
                        lhsT=w1_q[a][:, t * P : (t + 1) * P].bitcast(FP8X4),
                        lhsT_scale=w1_s[a][:, t * P : (t + 1) * P],
                        rhs=v_w[a][:, cols].bitcast(FP8X4),
                        rhs_scale=v_s[PACK * a :, cols],
                        start=(a == 0),
                        stop=(a == PASSES - 1),
                    )
                nc.scalar.activation(out=h[t][:, cols], in_=acc[:], func=ACT.Identity, bias=bias[:, t : t + 1])

        before = keep.tile([P, PACK, S], F32, name="before", tag="tab_w0")

        def fetch_before(t):
            nc.vector.tensor_copy(before[:, t, :], page[t][:].indirect(idx4[:]))

        def put(t, cols):
            nc.vector.tensor_tensor(page[t][:].indirect(entries(idx2, cols)), h[t][:, cols], gain[t][:, cols], ALU.mult)

        fetch_before(0)
        put(0, slice(0, BANK))
        fetch_before(1)
        put(0, slice(BANK, S))
        for t in range(1, PACK):
            if t + 1 < PACK:
                fetch_before(t + 1)
            put(t, slice(0, S))

        twice_sq = keep.tile([P, BLOCKS, S], F32, name="twice_sq")
        entry_blocks = BANK // P
        for c in range(CHUNKS):
            mag = keep.tile([P, entry_blocks, N], F32, name="mag", tag="mag", bufs=2)
            for e in range(entry_blocks):
                cols = slice(c * BANK + e * P, c * BANK + (e + 1) * P)
                ph = psum.tile([P, N], F32, name="ph", tag="ph", bufs=2)
                for n0, n1 in ((0, 2 * P), (2 * P, N)):
                    for a in range(PASSES):
                        nc.tensor.matmul_mx(
                            out=ph[:, n0:n1],
                            lhsT=v_w[a][:, cols].bitcast(FP8X4),
                            lhsT_scale=v_s[PACK * a :, cols],
                            rhs=w2_w[a][:, n0:n1].bitcast(FP8X4),
                            rhs_scale=w2_sc[PACK * a :, n0:n1],
                            start=(a == 0),
                            stop=(a == PASSES - 1),
                        )
                nc.scalar.activation(out=mag[:, e, :], in_=ph[:], func=ACT.Abs)
            turns = keep.tile([P, entry_blocks, N], U32, name="turns", tag="turns", bufs=2)
            nc.scalar.activation(out=turns[:], in_=mag[:], func=ACT.Copy, scale=1.0 / (2.0 * math.pi), bias=0.75)
            shift = keep.tile([P, entry_blocks, N], F32, name="shift", tag="shift", bufs=2)
            nc.scalar.activation(out=shift[:], in_=turns[:], func=ACT.Copy, scale=-2.0 * math.pi, bias=math.pi)
            for b in range(BLOCKS):
                red = psum.tile([P, BANK], F32, name="red", tag="red", bufs=2)
                for e in range(entry_blocks):
                    for first, term in ((True, mag), (False, shift)):
                        nc.tensor.matmul(
                            out=red[:, e * P : (e + 1) * P],
                            lhsT=term[:, e, b * P : (b + 1) * P],
                            rhs=ident[:],
                            is_transpose=True,
                            start=first,
                            stop=not first,
                        )
                half_cos = keep.tile([P, BANK], F32, name="half_cos", tag=("half_cos", "x_bf0")[(c * BLOCKS + b) % 2], align_bytes=64)
                nc.scalar.activation(out=half_cos[:], in_=red[:], func=ACT.Sin, scale=0.5)
                nc.scalar.activation(
                    out=twice_sq[:, b, c * BANK : (c + 1) * BANK], in_=half_cos[:], func=ACT.Square, scale=math.sqrt(2.0)
                )

        spans = (slice(0, 256), slice(256, 768), slice(768, 1024))
        after_tags = (f"gain{PACK - 1}", f"h{PACK - 1}", f"gain{PACK - 1}")
        score_tags = ("planes0", "score1", "score2")
        woven_tags = ("x_bf0", "planes0", "planes1")
        banks = [("acc", 4)] * 4 + [("red", 2)] * 2 + [("ph", 2)] * 2
        x_q, x_s = [], []
        for c, cols in enumerate(spans):
            width = cols.stop - cols.start
            picked = keep.tile([P, PACK, width], F32, name=f"after{c}", tag=after_tags[c], align_bytes=64)
            for t in range(PACK):
                nc.vector.tensor_copy(picked[:, t, :], page[t][:].indirect(entries(idx3, cols)))
            planes = keep.tile([P, PACK, width], BF16, name=f"planes{c}", tag=f"planes{c}", align_bytes=64)
            nc.vector.tensor_tensor(planes[:], picked[:], before[:, :, cols], ALU.max)
            x_bf = keep.tile([P, width, PACK], BF16, name=f"x_bf{c}", tag=woven_tags[c], align_bytes=64)
            nc.scalar.copy(out=x_bf[:], in_=planes[:].rearrange("p t j -> p j t"))
            codes = keep.tile([P, width], U32, name=f"x_q{c}", align_bytes=64)
            scales = keep.tile([P, width], U8, name=f"x_s{c}", align_bytes=64)
            nc.vector.quantize_mx(
                out=codes[:].bitcast(FP8X4), scales=scales[:], in_=x_bf[:].rearrange("p j t -> p (j t)")
            )
            x_q.append(codes)
            x_s.append(scales)
        for c, cols in enumerate(spans):
            width = cols.stop - cols.start
            score = keep.tile([P, BLOCKS, width], F32, name=f"score{c}", tag=score_tags[c], align_bytes=64)
            for b in range(BLOCKS):
                tag, bufs = banks[(c * BLOCKS + b) % len(banks)]
                acc = psum.tile([P, width], F32, name="y", tag=tag, bufs=bufs)
                nc.tensor.matmul_mx(
                    out=acc[:],
                    lhsT=w4_w[:, 2 * b * P : 2 * (b + 1) * P].bitcast(FP4X4),
                    lhsT_scale=w4_sc[:, b * P : (b + 1) * P],
                    rhs=x_q[c][:].bitcast(FP8X4),
                    rhs_scale=x_s[c][:],
                    start=True,
                    stop=True,
                )
                nc.vector.scalar_tensor_tensor(
                    score[:, b, :], twice_sq[:, b, cols], 1.0, acc[:], ALU.subtract, ALU.mult
                )
                nc.sync.dma_start(out=out[b * P : (b + 1) * P, cols], in_=score[:, b, :])
